import numpy as np
import ml_dtypes


def mxq(x, axis, fmt="e4m3"):
    dtype, down = {"e4m3": (ml_dtypes.float8_e4m3fn, 7), "e5m2": (ml_dtypes.float8_e5m2, 14)}[fmt]
    v = np.moveaxis(np.asarray(x, np.float32).astype(ml_dtypes.bfloat16).astype(np.float64), axis, -1)
    blocks = v.reshape(v.shape[:-1] + (-1, 32))
    amax = np.abs(blocks).max(-1, keepdims=True)
    byte = np.maximum(np.where(amax > 0, np.frexp(amax)[1] - 1 + 127, 0) - down, 1)
    scale = np.exp2(byte - 127.0)
    codes = (blocks / scale).astype(np.float32).astype(dtype).astype(np.float64)
    return np.moveaxis((codes * scale).reshape(v.shape), -1, axis)


WIDE = False


def mx_kscale(k):
    if not WIDE:
        return np.ones(k)
    levels = np.array([10, -10, 5, -5, 0])
    if k % 512:
        return np.exp2(np.random.permutation(np.resize(levels, k // 32))).repeat(32)
    a = np.empty((k // 512, 16))
    for p in range(k // 512):
        a[p, :8] = np.random.permutation(np.resize(levels, 8))
        for g in range(8):
            far = levels[np.abs(levels - a[p, g]) >= 10]
            a[p, g + 8] = far[np.random.randint(len(far))]
    return np.exp2(a.ravel()).repeat(32)


def f64(x):
    return np.asarray(x).astype(np.float64)


def striped(idx):
    return np.tile(idx.reshape(-1, 16).T, (8, 1)).astype(np.uint16)


def unstriped(offs):
    return offs[:16].T.reshape(-1).astype(np.int64)


def striped8(idx):
    return np.concatenate([x.reshape(-1, 16).T for x in idx]).astype(np.uint16)


def runs(offs, k):
    lists = np.stack([offs[16 * r : 16 * r + 16].T.reshape(-1) for r in range(8)]).astype(np.int64)
    return lists[np.arange(k) % 512 // 64]


def pack_weight(w):
    k, n = w.shape
    w = f64(np.asarray(w, np.float32).astype(ml_dtypes.bfloat16)).reshape(k // 32, 32, n)
    amax = np.abs(w).max(1)
    byte = np.clip(np.where(amax > 0, np.frexp(amax)[1] - 1 + 127 - 7, 1), 1, 254)
    scaled = (w * np.exp2(127.0 - byte)[:, None, :]).reshape(k, n).astype(np.float32)
    words = np.ascontiguousarray(scaled.reshape(k // 512, 128, 4, n).transpose(0, 1, 3, 2)).astype(ml_dtypes.float8_e4m3fn).view(np.uint8)
    return words, np.ascontiguousarray(byte.astype(np.uint8).reshape(k // 512, 16, n))


def unpack_weight(words, scales):
    g, p, n, _ = words.shape
    vals = np.ascontiguousarray(words).view(ml_dtypes.float8_e4m3fn).astype(np.float64) * np.repeat(np.exp2(scales.astype(np.float64) - 127.0), 8, axis=1)[..., None]
    return vals.transpose(0, 1, 3, 2).reshape(g * 512, n)

def planes(y):
    n, m = y.shape
    v = y.astype(np.float32).astype(ml_dtypes.bfloat16).astype(np.float64).reshape(n // 32, 32, m)
    top = np.abs(v).max(1)
    byte = np.clip(np.where(top > 0, np.frexp(top)[1] - 1 + 127 - 7, 1), 1, 254)
    codes = (v * np.exp2(127.0 - byte)[:, None, :]).reshape(n, m).astype(np.float32).astype(ml_dtypes.float8_e4m3fn).view(np.uint8)
    words = codes.reshape(n // 512, 128, 4, m).transpose(0, 1, 3, 2)
    return np.ascontiguousarray(words), np.ascontiguousarray(byte.astype(np.uint8).reshape(n // 512, 16, m))


K, T, S, N, H = 512, 2048, 512, 512, 512


def setup_inputs():
    n = np.random.standard_normal
    s = mx_kscale(K)[:, None]
    u = mx_kscale(H)
    packed_xT = pack_weight(n((K, T)) * s)
    packed_w1 = pack_weight(n((K, H)) / np.sqrt(K) / s)
    packed_w2 = pack_weight(n((H, N)) / np.sqrt(H) / u[:, None])
    return {
        "x_words": packed_xT[0],
        "x_scales": packed_xT[1],
        "w1_words": packed_w1[0],
        "w1_scales": packed_w1[1],
        "gn": (np.random.uniform(0.5, 1.5, (H, 1)) * u[:, None]).astype(np.float32),
        "w2_words": packed_w2[0],
        "w2_scales": packed_w2[1],
        "offs": striped(np.random.permutation(T)[:S]),
        "p1": striped8(np.stack([np.random.permutation(S) for _ in range(8)])),
        "p2": striped8(np.stack([np.random.permutation(S) for _ in range(8)])),
    }


def reference(x_words, x_scales, w1_words, w1_scales, gn, w2_words, w2_scales, offs, p1, p2):
    xq = unpack_weight(x_words, x_scales)[:, unstriped(offs)]
    y = unpack_weight(w1_words, w1_scales).T @ xq
    d1 = y[np.arange(H)[:, None], runs(p1, H)] - y
    d2 = y[np.arange(H)[:, None], runs(p2, H)] - y
    z = f64(gn) * (y + 0.25 * ((np.exp(-0.5 * ((d1) ** 2))) * d1) + 0.25 * ((np.exp(-0.5 * ((d2) ** 2))) * d2))
    out_0 = unpack_weight(w2_words, w2_scales).T @ mxq(z, 0, "e4m3")
    return (out_0,) + planes(out_0)

@@ -1,0 +1,285 @@
+from contextlib import ExitStack
+
+import concourse.mybir as mybir
+from concourse.masks import make_identity
+
+F32 = mybir.dt.float32
+BF16 = mybir.dt.bfloat16
+I32 = mybir.dt.int32
+U32 = mybir.dt.uint32
+U16 = mybir.dt.uint16
+U8 = mybir.dt.uint8
+FP8X4 = mybir.dt.float8_e4m3fn_x4
+ALU = mybir.AluOpType
+ACT = mybir.ActivationFunctionType
+
+P = 128
+PACK = 4
+T = 2048
+S = 512
+HALF = 256
+FLOPS = 2 * 2 * 512 * 512 * 512
+
+CHUNKS = [256,128,128]
+DBUFS = 3
+DIRECT = [0,0,1]
+TWIN = ["dve","act","act","act"]
+GY = "dve"
+OUTIL = ["dve","dve","psum"]
+POST = [[4,5,6],[8,9,13],[11,12,13]]
+WAT = [0,0,1,2]
+ALIAS = 1
+SPLITLAST = 1
+ZT = ["act","act","act"]
+
+
+def tile_picked_perona_none_po_kernel(
+    tc, x_words, x_scales, w1_words, w1_scales, gn, w2_words, w2_scales, offs, p1, p2, out_0, out_1, out_2
+):
+    nc = tc.nc
+    with ExitStack() as ctx:
+        keep = ctx.enter_context(tc.tile_pool(name="keep", bufs=1))
+        work = ctx.enter_context(tc.tile_pool(name="work", bufs=DBUFS))
+        chunk = ctx.enter_context(tc.tile_pool(name="chunk", bufs=3))
+        ps_a = ctx.enter_context(tc.psum_pool(name="ps_a", bufs=4))
+        ps_w = ctx.enter_context(tc.psum_pool(name="ps_w", bufs=1))
+        ps_o = ctx.enter_context(tc.psum_pool(name="ps_o", bufs=3))
+
+        def words_of(ap):
+            return ap[0].rearrange("p n t -> p (n t)").bitcast(I32)
+
+        offs_t = keep.tile([P, S // 16], U16, name="offs_t")
+        p1_t = keep.tile([P, S // 16], U16, name="p1_t")
+        p2_t = keep.tile([P, S // 16], U16, name="p2_t")
+        xw = keep.tile([P, T], I32, name="xw", align_bytes=64)
+        xs = keep.tile([P, T], U8, name="xs", tag="xs", align_bytes=64)
+        ww = keep.tile([P, S], I32, name="ww", align_bytes=64)
+        ws = keep.tile([P, S], U8, name="ws", align_bytes=64)
+        gn_t = keep.tile([P, PACK], F32, name="gn_t")
+        ident = keep.tile([P, P], F32, name="ident", align_bytes=64)
+
+        nc.gpsimd.memset(xs[:].bitcast(I32), 0)
+        nc.gpsimd.memset(ws[:].bitcast(I32), 0)
+
+        def load_scales(queues, dst, src):
+            for q, queue in enumerate(queues):
+                queue.dma_start(out=dst[32 * q : 32 * q + 4, :].bitcast(I32), in_=src[0, 4 * q : 4 * q + 4, :].bitcast(I32))
+
+        nc.sync.dma_start(offs_t[:], offs)
+        nc.sync.dma_start(p1_t[:], p1)
+        nc.sync.dma_start(p2_t[:], p2)
+        nc.sync.dma_start(out=ww[:], in_=words_of(w1_words))
+        nc.sync.dma_start(out=xw[:], in_=words_of(x_words))
+        load_scales([nc.scalar] * 4, xs, x_scales)
+        load_scales([nc.gpsimd, nc.gpsimd, nc.scalar, nc.scalar], ws, w1_scales)
+        nc.gpsimd.dma_start(out=gn_t[:], in_=gn.rearrange("(p t) o -> p (t o)", t=PACK))
+        make_identity(nc, ident[:])
+
+        def deal(name):
+            dw = keep.tile([P, S], I32, name=name + "w", align_bytes=64)
+            ds = keep.tile([P, S], U8, name=name + "s", align_bytes=64)
+            nc.vector.tensor_copy(
+                out=dw[:].rearrange("p (t a b) -> p a t b", t=PACK, b=4),
+                in_=ww[:].rearrange("p (a b t) -> p a t b", t=PACK, b=4),
+            )
+            nc.gpsimd.tensor_copy(
+                out=ds[:].rearrange("p (t m) -> p t m", t=PACK),
+                in_=ws[:].rearrange("p (m t) -> p t m", t=PACK),
+            )
+            return dw, ds
+
+        w1dw, w1ds = deal("w1d")
+        nc.sync.dma_start(out=ww[:], in_=words_of(w2_words))
+        load_scales([nc.sync] * 4, ws, w2_scales)
+
+        xgs = keep.tile([P, S], U8, name="xgs", align_bytes=64)
+        nc.vector.tensor_copy(out=xgs[:], in_=xs[:].indirect(offs_t[:]))
+        xgw = keep.tile([P, S], U32, name="xgw", tag=("xs" if ALIAS else "xgw"), align_bytes=64)
+        for h in range(2):
+            nc.vector.tensor_copy(out=xgw[:, h * HALF : (h + 1) * HALF], in_=xw[:].bitcast(U32).indirect(offs_t[:, h * 16 : (h + 1) * 16]))
+
+        gn4 = keep.tile([P, PACK], F32, name="gn4")
+        nc.gpsimd.tensor_scalar(out=gn4[:], in0=gn_t[:], scalar1=0.25, scalar2=0.0, op0=ALU.mult, op1=ALU.add)
+
+        y = [keep.tile([P, S], F32, name="y%d" % t, align_bytes=64) for t in range(PACK)]
+        y2 = [keep.tile([P, S], F32, name="ytwin%d" % t, align_bytes=64) for t in range(PACK)]
+        gy = [keep.tile([P, S], F32, name="gy%d" % t, align_bytes=64) for t in range(PACK)]
+        gy_cols = sum(w for w, d in zip(CHUNKS, DIRECT) if not d)
+        y_banks = {}
+        for t in range(PACK):
+            cols = slice(t * P, (t + 1) * P)
+            for a, b in ([(0, HALF), (HALF, S)] if t == 0 else [(0, S)]):
+                if a == 0 and t == 0:
+                    bank = ps_o.tile([P, b - a], F32, name="y_bank", tag="o")
+                else:
+                    bank = ps_a.tile([P, b - a], F32, name="y_bank", tag="a")
+                nc.tensor.matmul_mx(
+                    out=bank[:], lhsT=w1dw[:, cols].bitcast(FP8X4), lhsT_scale=w1ds[:, cols],
+                    rhs=xgw[:, a:b].bitcast(FP8X4), rhs_scale=xgs[:, a:b], start=True, stop=True,
+                )
+                y_banks[t, a] = bank
+
+        def window(t):
+            for a, b in ([(0, HALF), (HALF, S)] if t == 0 else [(0, S)]):
+                nc.scalar.copy(out=y[t][:, a:b], in_=y_banks[t, a][:])
+                if a == 0:
+                    if TWIN[t] == "dve":
+                        nc.vector.tensor_copy(out=y2[t][:, :HALF], in_=y[t][:, :HALF])
+                    else:
+                        nc.scalar.copy(out=y2[t][:, :HALF], in_=y_banks[t, 0][:, :HALF])
+            nc.sync.dma_start(out=y2[t][:, HALF:], in_=y[t][:, HALF:])
+
+        def gained(t):
+            if GY == "dve":
+                nc.vector.tensor_scalar(out=gy[t][:, :gy_cols], in0=y[t][:, :gy_cols], scalar1=gn_t[:, t : t + 1], scalar2=None, op0=ALU.mult)
+            elif GY == "pool":
+                nc.gpsimd.tensor_scalar(out=gy[t][:, :gy_cols], in0=y[t][:, :gy_cols], scalar1=gn_t[:, t : t + 1], scalar2=0.0, op0=ALU.mult, op1=ALU.add)
+            else:
+                nc.scalar.activation(out=gy[t][:, :gy_cols], in_=y[t][:, :gy_cols], func=ACT.Copy, scale=gn_t[:, t : t + 1])
+
+        out_codes = keep.tile([P, S], I32, name="out_codes", align_bytes=64)
+        out_scales = keep.tile([P, S], U8, name="out_scales", align_bytes=64)
+        out_rows = out_0.rearrange("(p t) j -> p t j", t=PACK)
+        out_words = words_of(out_1)
+
+        starts = [sum(CHUNKS[:c]) for c in range(len(CHUNKS))]
+        steps = [(c, t) for c in range(len(CHUNKS)) for t in range(PACK)]
+        zt_banks = {}
+        zsum = {}
+        state = {}
+
+        def gather(c, t, split):
+            c0, width = starts[c], CHUNKS[c]
+            d = work.tile([P, 2, width], F32, name="d", tag="d", align_bytes=64)
+            e = work.tile([P, 2, width], F32, name="e", tag="e", align_bytes=64)
+            cols = slice(c0, c0 + width)
+            lists = slice(c0 // 16, (c0 + width) // 16)
+            for l, lst in enumerate((p1_t, p2_t)):
+                nc.vector.tensor_tensor(out=d[:, l, :], in0=y[t][:].indirect(lst[:, lists]), in1=y2[t][:, cols], op=ALU.subtract)
+                if split:
+                    nc.scalar.activation(out=e[:, l, :], in_=d[:, l, :], func=ACT.Square)
+                    nc.scalar.activation(out=e[:, l, :], in_=e[:, l, :], func=ACT.Exp, scale=-0.5)
+            if not split:
+                nc.scalar.activation(out=e[:], in_=d[:], func=ACT.Square)
+                nc.scalar.activation(out=e[:], in_=e[:], func=ACT.Exp, scale=-0.5)
+            return d, e
+
+        def pull(c, t, split, d, e):
+            c0, width = starts[c], CHUNKS[c]
+            m = work.tile([P, 2, width], F32, name="m", tag="m", align_bytes=64)
+            if DIRECT[c]:
+                if t == 0:
+                    zsum[c] = chunk.tile([P, PACK, width], F32, name="zsum", tag="zsum", align_bytes=64)
+                part = work.tile([P, width], F32, name="part", tag="part", align_bytes=64)
+                if split:
+                    nc.vector.scalar_tensor_tensor(out=m[:, 0, :], in0=e[:, 0, :], scalar=gn4[:, t : t + 1], in1=d[:, 0, :], op0=ALU.mult, op1=ALU.mult)
+                    nc.vector.scalar_tensor_tensor(out=part[:], in0=y[t][:, c0 : c0 + width], scalar=gn_t[:, t : t + 1], in1=m[:, 0, :], op0=ALU.mult, op1=ALU.add)
+                    nc.vector.tensor_tensor(out=m[:, 1, :], in0=e[:, 1, :], in1=d[:, 1, :], op=ALU.mult)
+                    nc.vector.scalar_tensor_tensor(out=zsum[c][:, t, :], in0=m[:, 1, :], scalar=gn4[:, t : t + 1], in1=part[:], op0=ALU.mult, op1=ALU.add)
+                else:
+                    nc.vector.scalar_tensor_tensor(out=m[:], in0=e[:], scalar=gn4[:, t : t + 1], in1=d[:], op0=ALU.mult, op1=ALU.mult)
+                    nc.vector.scalar_tensor_tensor(out=part[:], in0=y[t][:, c0 : c0 + width], scalar=gn_t[:, t : t + 1], in1=m[:, 0, :], op0=ALU.mult, op1=ALU.add)
+                    nc.vector.tensor_tensor(out=zsum[c][:, t, :], in0=part[:], in1=m[:, 1, :], op=ALU.add)
+                return
+            nc.vector.scalar_tensor_tensor(out=m[:], in0=e[:], scalar=gn4[:, t : t + 1], in1=d[:], op0=ALU.mult, op1=ALU.mult)
+            for b in range(width // P):
+                key = c0 + b * P
+                if t == 0:
+                    zt_banks[key] = ps_a.tile([P, PACK, P], F32, name="zt_bank", tag="a")
+                terms = (gy[t][:, key : key + P], m[:, 0, b * P : (b + 1) * P], m[:, 1, b * P : (b + 1) * P])
+                for i, term in enumerate(terms):
+                    nc.tensor.matmul(zt_banks[key][:, t, :], lhsT=term, rhs=ident[:], is_transpose=True, start=(i == 0), stop=(i == 2))
+
+        def interleave(engine, dst, src):
+            dst = dst.rearrange("p (c i t) -> p c t i", i=4, t=PACK)
+            src = src.rearrange("p t (c i) -> p c t i", i=4)
+            if engine == "act":
+                nc.scalar.copy(out=dst, in_=src)
+            else:
+                nc.vector.tensor_copy(out=dst, in_=src)
+
+        def turn_back(c):
+            c0, width = starts[c], CHUNKS[c]
+            z = chunk.tile([P, width * PACK], BF16, name="z", tag="z", align_bytes=64)
+            state[c] = z
+            if DIRECT[c]:
+                interleave("dve", z[:], zsum[c][:])
+                return
+            nb = width // P
+            zw_bank = ps_w.tile([P, nb, 2, P], F32, name="zw_bank", tag="w")
+            for b in range(nb):
+                zt = chunk.tile([P, 2, P, 2], BF16, name="zt", tag="zt", align_bytes=64)
+                src = zt_banks[c0 + b * P][:].rearrange("c (u e) p -> c u p e", e=2)
+                if ZT[c] == "act":
+                    nc.scalar.copy(out=zt[:], in_=src)
+                else:
+                    nc.vector.tensor_copy(out=zt[:], in_=src)
+                pairs = zt[:].rearrange("c u p e -> c (u p e)").bitcast(F32)
+                for u in range(2):
+                    nc.tensor.transpose(zw_bank[:, b, u, :], pairs[:, u * P : (u + 1) * P], ident[:])
+            nc.scalar.copy(
+                out=z[:].bitcast(F32).rearrange("p (b c u) -> p b c u", b=nb, u=2),
+                in_=zw_bank[:].rearrange("p b u c -> p b c u"),
+            )
+
+        def second(c):
+            c0, width = starts[c], CHUNKS[c]
+            zc = chunk.tile([P, width], I32, name="zc", tag="zc", align_bytes=64)
+            zs = chunk.tile([P, width], U8, name="zs", tag="zs", align_bytes=64)
+            nc.vector.quantize_mx(out=zc[:].bitcast(FP8X4), scales=zs[:], in_=state[c][:])
+            res = chunk.tile([P, PACK, width], F32, name="res", tag="res", align_bytes=64)
+            rb = chunk.tile([P, width * PACK], BF16, name="rb", tag="rb", align_bytes=64)
+            per_bank = 2 if OUTIL[c] == "psum" else 512 // width
+            for t0 in range(0, PACK, per_bank):
+                bank = ps_o.tile([P, per_bank, width], F32, name="o_bank", tag="o")
+                for t in range(t0, t0 + per_bank):
+                    cols = slice(t * P, (t + 1) * P)
+                    nc.tensor.matmul_mx(
+                        out=bank[:, t - t0, :], lhsT=w2dw[:, cols].bitcast(FP8X4), lhsT_scale=w2ds[:, cols],
+                        rhs=zc[:].bitcast(FP8X4), rhs_scale=zs[:], start=True, stop=True,
+                    )
+                if OUTIL[c] == "psum":
+                    nc.vector.tensor_copy(
+                        out=rb[:].rearrange("p (c t) -> p c t", t=PACK)[:, :, t0 : t0 + 2], in_=bank[:].rearrange("p t c -> p c t")
+                    )
+                nc.scalar.copy(out=res[:, t0 : t0 + per_bank, :], in_=bank[:])
+                if OUTIL[c] == "psum":
+                    nc.scalar.dma_start(out=out_rows[:, t0 : t0 + 2, c0 : c0 + width], in_=res[:, t0 : t0 + 2, :])
+            if OUTIL[c] != "psum":
+                nc.sync.dma_start(out=out_rows[:, :, c0 : c0 + width], in_=res[:])
+            state[c] = (res, rb)
+
+        def planes(c):
+            c0, width = starts[c], CHUNKS[c]
+            cols = slice(c0, c0 + width)
+            res, rb = state[c]
+            if OUTIL[c] != "psum":
+                interleave(OUTIL[c], rb[:], res[:])
+            nc.vector.quantize_mx(out=out_codes[:, cols].bitcast(FP8X4), scales=out_scales[:, cols], in_=rb[:])
+            nc.sync.dma_start(out=out_words[:, cols], in_=out_codes[:, cols])
+
+        stages = (turn_back, second, planes)
+        lag = DBUFS - 1
+        n = len(steps)
+        held = {}
+        for i in range(n + lag + 4):
+            for t in range(PACK):
+                if WAT[t] == i:
+                    window(t)
+            if i == 1:
+                w2dw, w2ds = deal("w2d")
+            if i < n:
+                held[i] = gather(*steps[i], SPLITLAST and i == n - 1)
+            if i < PACK and gy_cols:
+                gained(i)
+            j = i - lag
+            if 0 <= j < n:
+                pull(*steps[j], SPLITLAST and j == n - 1, *held[j])
+            for c in reversed(range(len(CHUNKS))):
+                for k in range(3):
+                    if min(POST[c][k] + lag, n + lag + 3) == i:
+                        stages[k](c)
+
+        for q in range(4):
+            queue = nc.sync if q % 2 == 0 else nc.scalar
+            queue.dma_start(out=out_2[0, 4 * q : 4 * q + 4, :].bitcast(I32), in_=out_scales[32 * q : 32 * q + 4, :].bitcast(I32))

@@ -24,11 +24,11 @@ CHUNKS = [256,128,128]
 DBUFS = 3
 DIRECT = [0,0,1]
 TWIN = ["dve","act","act","act"]
-GY = "dve"
-OUTIL = ["dve","dve","psum"]
-POST = [[4,5,6],[8,9,13],[11,12,13]]
+GY = "daaa"
+OUTIL = ["act","act","psum"]
+POST = [[5,7,14],[9,14,14],[11,12,13]]
 WAT = [0,0,1,2]
-ALIAS = 1
+ALIAS = 0
 SPLITLAST = 1
 ZT = ["act","act","act"]
 
@@ -51,7 +51,7 @@ def tile_picked_perona_none_po_kernel(
         offs_t = keep.tile([P, S // 16], U16, name="offs_t")
         p1_t = keep.tile([P, S // 16], U16, name="p1_t")
         p2_t = keep.tile([P, S // 16], U16, name="p2_t")
-        xw = keep.tile([P, T], I32, name="xw", align_bytes=64)
+        xw = keep.tile([P, T], I32, name="xw", tag="xw", align_bytes=64)
         xs = keep.tile([P, T], U8, name="xs", tag="xs", align_bytes=64)
         ww = keep.tile([P, S], I32, name="ww", align_bytes=64)
         ws = keep.tile([P, S], U8, name="ws", align_bytes=64)
@@ -65,30 +65,30 @@ def tile_picked_perona_none_po_kernel(
             for q, queue in enumerate(queues):
                 queue.dma_start(out=dst[32 * q : 32 * q + 4, :].bitcast(I32), in_=src[0, 4 * q : 4 * q + 4, :].bitcast(I32))
 
+        nc.scalar.dma_start(out=gn_t[:], in_=gn.rearrange("(p t) o -> p (t o)", t=PACK))
         nc.sync.dma_start(offs_t[:], offs)
         nc.sync.dma_start(p1_t[:], p1)
         nc.sync.dma_start(p2_t[:], p2)
         nc.sync.dma_start(out=ww[:], in_=words_of(w1_words))
         nc.sync.dma_start(out=xw[:], in_=words_of(x_words))
         load_scales([nc.scalar] * 4, xs, x_scales)
-        load_scales([nc.gpsimd, nc.gpsimd, nc.scalar, nc.scalar], ws, w1_scales)
-        nc.gpsimd.dma_start(out=gn_t[:], in_=gn.rearrange("(p t) o -> p (t o)", t=PACK))
+        load_scales([nc.gpsimd, nc.scalar, nc.scalar, nc.scalar], ws, w1_scales)
         make_identity(nc, ident[:])
 
-        def deal(name):
-            dw = keep.tile([P, S], I32, name=name + "w", align_bytes=64)
+        def deal(name, tag):
+            dw = keep.tile([P, S], I32, name=name + "w", tag=tag, align_bytes=64)
             ds = keep.tile([P, S], U8, name=name + "s", align_bytes=64)
             nc.vector.tensor_copy(
                 out=dw[:].rearrange("p (t a b) -> p a t b", t=PACK, b=4),
                 in_=ww[:].rearrange("p (a b t) -> p a t b", t=PACK, b=4),
             )
-            nc.gpsimd.tensor_copy(
+            nc.vector.tensor_copy(
                 out=ds[:].rearrange("p (t m) -> p t m", t=PACK),
                 in_=ws[:].rearrange("p (m t) -> p t m", t=PACK),
             )
             return dw, ds
 
-        w1dw, w1ds = deal("w1d")
+        w1dw, w1ds = deal("w1d", "w1d")
         nc.sync.dma_start(out=ww[:], in_=words_of(w2_words))
         load_scales([nc.sync] * 4, ws, w2_scales)
 
@@ -99,7 +99,7 @@ def tile_picked_perona_none_po_kernel(
             nc.vector.tensor_copy(out=xgw[:, h * HALF : (h + 1) * HALF], in_=xw[:].bitcast(U32).indirect(offs_t[:, h * 16 : (h + 1) * 16]))
 
         gn4 = keep.tile([P, PACK], F32, name="gn4")
-        nc.gpsimd.tensor_scalar(out=gn4[:], in0=gn_t[:], scalar1=0.25, scalar2=0.0, op0=ALU.mult, op1=ALU.add)
+        nc.vector.tensor_scalar(out=gn4[:], in0=gn_t[:], scalar1=0.25, scalar2=0.0, op0=ALU.mult, op1=ALU.add)
 
         y = [keep.tile([P, S], F32, name="y%d" % t, align_bytes=64) for t in range(PACK)]
         y2 = [keep.tile([P, S], F32, name="ytwin%d" % t, align_bytes=64) for t in range(PACK)]
@@ -130,9 +130,9 @@ def tile_picked_perona_none_po_kernel(
             nc.sync.dma_start(out=y2[t][:, HALF:], in_=y[t][:, HALF:])
 
         def gained(t):
-            if GY == "dve":
+            if GY[t] == "d":
                 nc.vector.tensor_scalar(out=gy[t][:, :gy_cols], in0=y[t][:, :gy_cols], scalar1=gn_t[:, t : t + 1], scalar2=None, op0=ALU.mult)
-            elif GY == "pool":
+            elif GY[t] == "p":
                 nc.gpsimd.tensor_scalar(out=gy[t][:, :gy_cols], in0=y[t][:, :gy_cols], scalar1=gn_t[:, t : t + 1], scalar2=0.0, op0=ALU.mult, op1=ALU.add)
             else:
                 nc.scalar.activation(out=gy[t][:, :gy_cols], in_=y[t][:, :gy_cols], func=ACT.Copy, scale=gn_t[:, t : t + 1])
@@ -191,8 +191,8 @@ def tile_picked_perona_none_po_kernel(
                     nc.tensor.matmul(zt_banks[key][:, t, :], lhsT=term, rhs=ident[:], is_transpose=True, start=(i == 0), stop=(i == 2))
 
         def interleave(engine, dst, src):
-            dst = dst.rearrange("p (c i t) -> p c t i", i=4, t=PACK)
-            src = src.rearrange("p t (c i) -> p c t i", i=4)
+            dst = dst.rearrange("p (c t) -> p c t", t=PACK)
+            src = src.rearrange("p t c -> p c t")
             if engine == "act":
                 nc.scalar.copy(out=dst, in_=src)
             else:
@@ -267,7 +267,7 @@ def tile_picked_perona_none_po_kernel(
                 if WAT[t] == i:
                     window(t)
             if i == 1:
-                w2dw, w2ds = deal("w2d")
+                w2dw, w2ds = deal("w2d", "xw")
             if i < n:
                 held[i] = gather(*steps[i], SPLITLAST and i == n - 1)
             if i < PACK and gy_cols:

@@ -17,20 +17,16 @@ P = 128
 PACK = 4
 T = 2048
 S = 512
-HALF = 256
-FLOPS = 2 * 2 * 512 * 512 * 512
+HALF = S // 2
+BANK = 512
+PER_COLUMN = 16
+FLOPS = 2 * 2 * S * S * S
 
-CHUNKS = [256,128,128]
-DBUFS = 3
-DIRECT = [0,0,1]
-TWIN = ["dve","act","act","act"]
-GY = "daaa"
-OUTIL = ["act","act","psum"]
-POST = [[5,7,14],[9,14,14],[11,12,13]]
-WAT = [0,0,1,2]
-ALIAS = 0
-SPLITLAST = 1
-ZT = ["act","act","act"]
+CHUNKS = [(0, HALF), (HALF, P), (HALF + P, P)]
+LAST = len(CHUNKS) - 1
+STEPS = [(t, 0, HALF) for t in range(PACK)] + [(0, HALF, HALF)]
+STEPS = STEPS + [(t, first, width) for first, width in CHUNKS[1:] for t in range(1, PACK)]
+AHEAD = 3
 
 
 def tile_picked_perona_none_po_kernel(
@@ -39,247 +35,243 @@ def tile_picked_perona_none_po_kernel(
     nc = tc.nc
     with ExitStack() as ctx:
         keep = ctx.enter_context(tc.tile_pool(name="keep", bufs=1))
-        work = ctx.enter_context(tc.tile_pool(name="work", bufs=DBUFS))
-        chunk = ctx.enter_context(tc.tile_pool(name="chunk", bufs=3))
-        ps_a = ctx.enter_context(tc.psum_pool(name="ps_a", bufs=4))
-        ps_w = ctx.enter_context(tc.psum_pool(name="ps_w", bufs=1))
-        ps_o = ctx.enter_context(tc.psum_pool(name="ps_o", bufs=3))
+        per_chunk = ctx.enter_context(tc.tile_pool(name="per_chunk", bufs=len(CHUNKS)))
+        ps_sum = ctx.enter_context(tc.psum_pool(name="ps_sum", bufs=4))
+        ps_pairs = ctx.enter_context(tc.psum_pool(name="ps_pairs", bufs=1))
+        ps_out = ctx.enter_context(tc.psum_pool(name="ps_out", bufs=3))
 
-        def words_of(ap):
-            return ap[0].rearrange("p n t -> p (n t)").bitcast(I32)
+        def words_of(packed):
+            return packed[0].rearrange("p n t -> p (n t)").bitcast(I32)
 
-        offs_t = keep.tile([P, S // 16], U16, name="offs_t")
-        p1_t = keep.tile([P, S // 16], U16, name="p1_t")
-        p2_t = keep.tile([P, S // 16], U16, name="p2_t")
-        xw = keep.tile([P, T], I32, name="xw", tag="xw", align_bytes=64)
-        xs = keep.tile([P, T], U8, name="xs", tag="xs", align_bytes=64)
-        ww = keep.tile([P, S], I32, name="ww", align_bytes=64)
-        ws = keep.tile([P, S], U8, name="ws", align_bytes=64)
-        gn_t = keep.tile([P, PACK], F32, name="gn_t")
+        def load_scales(queues, plane, scales):
+            for q, queue in enumerate(queues):
+                queue.dma_start(
+                    out=plane[32 * q : 32 * q + 4, :].bitcast(I32), in_=scales[0, 4 * q : 4 * q + 4, :].bitcast(I32)
+                )
+
+        offs_t = keep.tile([P, S // PER_COLUMN], U16, name="offs_t")
+        p1_t = keep.tile([P, S // PER_COLUMN], U16, name="p1_t")
+        p2_t = keep.tile([P, S // PER_COLUMN], U16, name="p2_t")
+        x_w = keep.tile([P, T], I32, name="x_w", tag="x_w", align_bytes=64)
+        x_s = keep.tile([P, T], U8, name="x_s", align_bytes=64)
+        raw_w = keep.tile([P, S], I32, name="raw_w", align_bytes=64)
+        raw_s = keep.tile([P, S], U8, name="raw_s", align_bytes=64)
+        gain = keep.tile([P, PACK], F32, name="gain")
         ident = keep.tile([P, P], F32, name="ident", align_bytes=64)
 
-        nc.gpsimd.memset(xs[:].bitcast(I32), 0)
-        nc.gpsimd.memset(ws[:].bitcast(I32), 0)
+        nc.gpsimd.memset(x_s[:].bitcast(I32), 0)
+        nc.gpsimd.memset(raw_s[:].bitcast(I32), 0)
 
-        def load_scales(queues, dst, src):
-            for q, queue in enumerate(queues):
-                queue.dma_start(out=dst[32 * q : 32 * q + 4, :].bitcast(I32), in_=src[0, 4 * q : 4 * q + 4, :].bitcast(I32))
-
-        nc.scalar.dma_start(out=gn_t[:], in_=gn.rearrange("(p t) o -> p (t o)", t=PACK))
+        nc.scalar.dma_start(out=gain[:], in_=gn.rearrange("(p t) o -> p (t o)", t=PACK))
         nc.sync.dma_start(offs_t[:], offs)
         nc.sync.dma_start(p1_t[:], p1)
         nc.sync.dma_start(p2_t[:], p2)
-        nc.sync.dma_start(out=ww[:], in_=words_of(w1_words))
-        nc.sync.dma_start(out=xw[:], in_=words_of(x_words))
-        load_scales([nc.scalar] * 4, xs, x_scales)
-        load_scales([nc.gpsimd, nc.scalar, nc.scalar, nc.scalar], ws, w1_scales)
+        nc.sync.dma_start(out=raw_w[:], in_=words_of(w1_words))
+        nc.sync.dma_start(out=x_w[:], in_=words_of(x_words))
+        load_scales([nc.scalar] * 4, x_s, x_scales)
+        load_scales([nc.gpsimd, nc.scalar, nc.scalar, nc.scalar], raw_s, w1_scales)
         make_identity(nc, ident[:])
 
         def deal(name, tag):
-            dw = keep.tile([P, S], I32, name=name + "w", tag=tag, align_bytes=64)
-            ds = keep.tile([P, S], U8, name=name + "s", align_bytes=64)
+            words = keep.tile([P, S], I32, name=name + "_w", tag=tag, align_bytes=64)
+            scales = keep.tile([P, S], U8, name=name + "_s", align_bytes=64)
             nc.vector.tensor_copy(
-                out=dw[:].rearrange("p (t a b) -> p a t b", t=PACK, b=4),
-                in_=ww[:].rearrange("p (a b t) -> p a t b", t=PACK, b=4),
+                out=words[:].rearrange("p (t a b) -> p a t b", t=PACK, b=4),
+                in_=raw_w[:].rearrange("p (a b t) -> p a t b", t=PACK, b=4),
             )
             nc.vector.tensor_copy(
-                out=ds[:].rearrange("p (t m) -> p t m", t=PACK),
-                in_=ws[:].rearrange("p (m t) -> p t m", t=PACK),
+                out=scales[:].rearrange("p (t m) -> p t m", t=PACK), in_=raw_s[:].rearrange("p (m t) -> p t m", t=PACK)
             )
-            return dw, ds
+            return words, scales
 
-        w1dw, w1ds = deal("w1d", "w1d")
-        nc.sync.dma_start(out=ww[:], in_=words_of(w2_words))
-        load_scales([nc.sync] * 4, ws, w2_scales)
+        w1_w, w1_s = deal("w1", "w1_w")
+        nc.sync.dma_start(out=raw_w[:], in_=words_of(w2_words))
+        load_scales([nc.sync] * 4, raw_s, w2_scales)
 
-        xgs = keep.tile([P, S], U8, name="xgs", align_bytes=64)
-        nc.vector.tensor_copy(out=xgs[:], in_=xs[:].indirect(offs_t[:]))
-        xgw = keep.tile([P, S], U32, name="xgw", tag=("xs" if ALIAS else "xgw"), align_bytes=64)
-        for h in range(2):
-            nc.vector.tensor_copy(out=xgw[:, h * HALF : (h + 1) * HALF], in_=xw[:].bitcast(U32).indirect(offs_t[:, h * 16 : (h + 1) * 16]))
+        halves = [slice(0, HALF), slice(HALF, S)]
+        picked_s = keep.tile([P, S], U8, name="picked_s", align_bytes=64)
+        picked_w = keep.tile([P, S], U32, name="picked_w", align_bytes=64)
+        nc.vector.tensor_copy(out=picked_s[:], in_=x_s[:].indirect(offs_t[:]))
+        for cells in halves:
+            entries = slice(cells.start // PER_COLUMN, cells.stop // PER_COLUMN)
+            nc.vector.tensor_copy(out=picked_w[:, cells], in_=x_w[:].bitcast(U32).indirect(offs_t[:, entries]))
 
-        gn4 = keep.tile([P, PACK], F32, name="gn4")
-        nc.vector.tensor_scalar(out=gn4[:], in0=gn_t[:], scalar1=0.25, scalar2=0.0, op0=ALU.mult, op1=ALU.add)
+        quarter_gain = keep.tile([P, PACK], F32, name="quarter_gain")
+        nc.vector.tensor_scalar(out=quarter_gain[:], in0=gain[:], scalar1=0.25, scalar2=0.0, op0=ALU.mult, op1=ALU.add)
 
         y = [keep.tile([P, S], F32, name="y%d" % t, align_bytes=64) for t in range(PACK)]
-        y2 = [keep.tile([P, S], F32, name="ytwin%d" % t, align_bytes=64) for t in range(PACK)]
-        gy = [keep.tile([P, S], F32, name="gy%d" % t, align_bytes=64) for t in range(PACK)]
-        gy_cols = sum(w for w, d in zip(CHUNKS, DIRECT) if not d)
-        y_banks = {}
-        for t in range(PACK):
-            cols = slice(t * P, (t + 1) * P)
-            for a, b in ([(0, HALF), (HALF, S)] if t == 0 else [(0, S)]):
-                if a == 0 and t == 0:
-                    bank = ps_o.tile([P, b - a], F32, name="y_bank", tag="o")
-                else:
-                    bank = ps_a.tile([P, b - a], F32, name="y_bank", tag="a")
-                nc.tensor.matmul_mx(
-                    out=bank[:], lhsT=w1dw[:, cols].bitcast(FP8X4), lhsT_scale=w1ds[:, cols],
-                    rhs=xgw[:, a:b].bitcast(FP8X4), rhs_scale=xgs[:, a:b], start=True, stop=True,
-                )
-                y_banks[t, a] = bank
+        y_twin = [keep.tile([P, S], F32, name="y_twin%d" % t, align_bytes=64) for t in range(PACK)]
+        gained_y = [keep.tile([P, S], F32, name="gained_y%d" % t, align_bytes=64) for t in range(PACK)]
 
-        def window(t):
-            for a, b in ([(0, HALF), (HALF, S)] if t == 0 else [(0, S)]):
-                nc.scalar.copy(out=y[t][:, a:b], in_=y_banks[t, a][:])
-                if a == 0:
-                    if TWIN[t] == "dve":
-                        nc.vector.tensor_copy(out=y2[t][:, :HALF], in_=y[t][:, :HALF])
-                    else:
-                        nc.scalar.copy(out=y2[t][:, :HALF], in_=y_banks[t, 0][:, :HALF])
-            nc.sync.dma_start(out=y2[t][:, HALF:], in_=y[t][:, HALF:])
+        def multiply(bank, words, scales, t, moving_words, moving_scales):
+            columns = slice(t * P, (t + 1) * P)
+            nc.tensor.matmul_mx(
+                out=bank, lhsT=words[:, columns].bitcast(FP8X4), lhsT_scale=scales[:, columns],
+                rhs=moving_words.bitcast(FP8X4), rhs_scale=moving_scales, start=True, stop=True,
+            )
 
-        def gained(t):
-            if GY[t] == "d":
-                nc.vector.tensor_scalar(out=gy[t][:, :gy_cols], in0=y[t][:, :gy_cols], scalar1=gn_t[:, t : t + 1], scalar2=None, op0=ALU.mult)
-            elif GY[t] == "p":
-                nc.gpsimd.tensor_scalar(out=gy[t][:, :gy_cols], in0=y[t][:, :gy_cols], scalar1=gn_t[:, t : t + 1], scalar2=0.0, op0=ALU.mult, op1=ALU.add)
+        y_banks = [
+            [ps_out.tile([P, HALF], F32, name="y_bank", tag="out"), ps_sum.tile([P, HALF], F32, name="y_bank", tag="sum")]
+        ]
+        for bank, cells in zip(y_banks[0], halves):
+            multiply(bank[:], w1_w, w1_s, 0, picked_w[:, cells], picked_s[:, cells])
+        for t in range(1, PACK):
+            y_banks.append(ps_sum.tile([P, S], F32, name="y_bank", tag="sum"))
+            multiply(y_banks[t][:], w1_w, w1_s, t, picked_w[:], picked_s[:])
+
+        def fetch_y(t):
+            if t == 0:
+                nc.scalar.copy(out=y[0][:, halves[0]], in_=y_banks[0][0][:])
+                nc.vector.tensor_copy(out=y_twin[0][:, halves[0]], in_=y[0][:, halves[0]])
+                nc.scalar.copy(out=y[0][:, halves[1]], in_=y_banks[0][1][:])
             else:
-                nc.scalar.activation(out=gy[t][:, :gy_cols], in_=y[t][:, :gy_cols], func=ACT.Copy, scale=gn_t[:, t : t + 1])
+                nc.scalar.copy(out=y[t][:], in_=y_banks[t][:])
+                nc.scalar.copy(out=y_twin[t][:, halves[0]], in_=y_banks[t][:, halves[0]])
+            nc.sync.dma_start(out=y_twin[t][:, halves[1]], in_=y[t][:, halves[1]])
+
+        def gain_y(t):
+            cells = slice(0, CHUNKS[LAST][0])
+            nc.scalar.activation(out=gained_y[t][:, cells], in_=y[t][:, cells], func=ACT.Copy, scale=gain[:, t : t + 1])
+
+        scratch = [keep.tile([P, S], F32, name="scratch%d" % i, align_bytes=64) for i in range(len(STEPS) + AHEAD)]
+        last_cells = slice(CHUNKS[LAST][0], S)
+        last_z = keep.tile([P, PACK, P], F32, name="last_z", align_bytes=64)
+        sum_banks = {}
+
+        def differences(i):
+            t, first, width = STEPS[i]
+            d = scratch[i][:, : 2 * width].rearrange("p (l w) -> p l w", l=2)
+            square = scratch[i + AHEAD][:, : 2 * width].rearrange("p (l w) -> p l w", l=2)
+            e = keep.tile([P, 2, width], F32, name="e%d" % i, align_bytes=64)
+            entries = slice(first // PER_COLUMN, (first + width) // PER_COLUMN)
+            by_list = i == len(STEPS) - 1
+            for l, lists in enumerate((p1_t, p2_t)):
+                nc.vector.tensor_tensor(
+                    out=d[:, l, :], in0=y[t][:].indirect(lists[:, entries]), in1=y_twin[t][:, first : first + width],
+                    op=ALU.subtract,
+                )
+                if by_list:
+                    nc.scalar.activation(out=square[:, l, :], in_=d[:, l, :], func=ACT.Square)
+                    nc.scalar.activation(out=e[:, l, :], in_=square[:, l, :], func=ACT.Exp, scale=-0.5)
+            if not by_list:
+                nc.scalar.activation(out=square, in_=d, func=ACT.Square)
+                nc.scalar.activation(out=e[:], in_=square, func=ACT.Exp, scale=-0.5)
+            return d, e
+
+        def pulls(i, d, e):
+            t, first, width = STEPS[i]
+            pull = keep.tile([P, 2, width], F32, name="pull%d" % i, align_bytes=64)
+            g, g4 = gain[:, t : t + 1], quarter_gain[:, t : t + 1]
+            if i == len(STEPS) - 1:
+                part = keep.tile([P, P], F32, name="part%d" % i, align_bytes=64)
+                nc.vector.scalar_tensor_tensor(out=pull[:, 0, :], in0=e[:, 0, :], scalar=g4, in1=d[:, 0, :], op0=ALU.mult, op1=ALU.mult)
+                nc.vector.scalar_tensor_tensor(out=part[:], in0=y[t][:, last_cells], scalar=g, in1=pull[:, 0, :], op0=ALU.mult, op1=ALU.add)
+                nc.vector.tensor_tensor(out=pull[:, 1, :], in0=e[:, 1, :], in1=d[:, 1, :], op=ALU.mult)
+                nc.vector.scalar_tensor_tensor(out=last_z[:, t, :], in0=pull[:, 1, :], scalar=g4, in1=part[:], op0=ALU.mult, op1=ALU.add)
+                return
+            nc.vector.scalar_tensor_tensor(out=pull[:], in0=e[:], scalar=g4, in1=d, op0=ALU.mult, op1=ALU.mult)
+            for block in range(first, first + width, P):
+                mine = slice(block - first, block - first + P)
+                if block == last_cells.start:
+                    part = keep.tile([P, P], F32, name="part%d" % i, align_bytes=64)
+                    nc.vector.scalar_tensor_tensor(out=part[:], in0=y[t][:, last_cells], scalar=g, in1=pull[:, 0, mine], op0=ALU.mult, op1=ALU.add)
+                    nc.vector.tensor_tensor(out=last_z[:, t, :], in0=part[:], in1=pull[:, 1, mine], op=ALU.add)
+                    continue
+                if t == 0:
+                    sum_banks[block] = ps_sum.tile([P, PACK, P], F32, name="sum_bank", tag="sum")
+                terms = (pull[:, 0, mine], pull[:, 1, mine], gained_y[t][:, block : block + P])
+                for k, term in enumerate(terms):
+                    nc.tensor.matmul(
+                        sum_banks[block][:, t, :], lhsT=term, rhs=ident[:], is_transpose=True,
+                        start=(k == 0), stop=(k == len(terms) - 1),
+                    )
 
         out_codes = keep.tile([P, S], I32, name="out_codes", align_bytes=64)
         out_scales = keep.tile([P, S], U8, name="out_scales", align_bytes=64)
         out_rows = out_0.rearrange("(p t) j -> p t j", t=PACK)
-        out_words = words_of(out_1)
+        pair_banks, out_banks, results, rounded = {}, {}, {}, {}
 
-        starts = [sum(CHUNKS[:c]) for c in range(len(CHUNKS))]
-        steps = [(c, t) for c in range(len(CHUNKS)) for t in range(PACK)]
-        zt_banks = {}
-        zsum = {}
-        state = {}
-
-        def gather(c, t, split):
-            c0, width = starts[c], CHUNKS[c]
-            d = work.tile([P, 2, width], F32, name="d", tag="d", align_bytes=64)
-            e = work.tile([P, 2, width], F32, name="e", tag="e", align_bytes=64)
-            cols = slice(c0, c0 + width)
-            lists = slice(c0 // 16, (c0 + width) // 16)
-            for l, lst in enumerate((p1_t, p2_t)):
-                nc.vector.tensor_tensor(out=d[:, l, :], in0=y[t][:].indirect(lst[:, lists]), in1=y2[t][:, cols], op=ALU.subtract)
-                if split:
-                    nc.scalar.activation(out=e[:, l, :], in_=d[:, l, :], func=ACT.Square)
-                    nc.scalar.activation(out=e[:, l, :], in_=e[:, l, :], func=ACT.Exp, scale=-0.5)
-            if not split:
-                nc.scalar.activation(out=e[:], in_=d[:], func=ACT.Square)
-                nc.scalar.activation(out=e[:], in_=e[:], func=ACT.Exp, scale=-0.5)
-            return d, e
-
-        def pull(c, t, split, d, e):
-            c0, width = starts[c], CHUNKS[c]
-            m = work.tile([P, 2, width], F32, name="m", tag="m", align_bytes=64)
-            if DIRECT[c]:
-                if t == 0:
-                    zsum[c] = chunk.tile([P, PACK, width], F32, name="zsum", tag="zsum", align_bytes=64)
-                part = work.tile([P, width], F32, name="part", tag="part", align_bytes=64)
-                if split:
-                    nc.vector.scalar_tensor_tensor(out=m[:, 0, :], in0=e[:, 0, :], scalar=gn4[:, t : t + 1], in1=d[:, 0, :], op0=ALU.mult, op1=ALU.mult)
-                    nc.vector.scalar_tensor_tensor(out=part[:], in0=y[t][:, c0 : c0 + width], scalar=gn_t[:, t : t + 1], in1=m[:, 0, :], op0=ALU.mult, op1=ALU.add)
-                    nc.vector.tensor_tensor(out=m[:, 1, :], in0=e[:, 1, :], in1=d[:, 1, :], op=ALU.mult)
-                    nc.vector.scalar_tensor_tensor(out=zsum[c][:, t, :], in0=m[:, 1, :], scalar=gn4[:, t : t + 1], in1=part[:], op0=ALU.mult, op1=ALU.add)
-                else:
-                    nc.vector.scalar_tensor_tensor(out=m[:], in0=e[:], scalar=gn4[:, t : t + 1], in1=d[:], op0=ALU.mult, op1=ALU.mult)
-                    nc.vector.scalar_tensor_tensor(out=part[:], in0=y[t][:, c0 : c0 + width], scalar=gn_t[:, t : t + 1], in1=m[:, 0, :], op0=ALU.mult, op1=ALU.add)
-                    nc.vector.tensor_tensor(out=zsum[c][:, t, :], in0=part[:], in1=m[:, 1, :], op=ALU.add)
-                return
-            nc.vector.scalar_tensor_tensor(out=m[:], in0=e[:], scalar=gn4[:, t : t + 1], in1=d[:], op0=ALU.mult, op1=ALU.mult)
-            for b in range(width // P):
-                key = c0 + b * P
-                if t == 0:
-                    zt_banks[key] = ps_a.tile([P, PACK, P], F32, name="zt_bank", tag="a")
-                terms = (gy[t][:, key : key + P], m[:, 0, b * P : (b + 1) * P], m[:, 1, b * P : (b + 1) * P])
-                for i, term in enumerate(terms):
-                    nc.tensor.matmul(zt_banks[key][:, t, :], lhsT=term, rhs=ident[:], is_transpose=True, start=(i == 0), stop=(i == 2))
-
-        def interleave(engine, dst, src):
-            dst = dst.rearrange("p (c t) -> p c t", t=PACK)
-            src = src.rearrange("p t c -> p c t")
-            if engine == "act":
-                nc.scalar.copy(out=dst, in_=src)
-            else:
-                nc.vector.tensor_copy(out=dst, in_=src)
+        def interleave(copy, dst, src):
+            copy(out=dst.rearrange("p (c t) -> p c t", t=PACK), in_=src.rearrange("p t c -> p c t"))
 
         def turn_back(c):
-            c0, width = starts[c], CHUNKS[c]
-            z = chunk.tile([P, width * PACK], BF16, name="z", tag="z", align_bytes=64)
-            state[c] = z
-            if DIRECT[c]:
-                interleave("dve", z[:], zsum[c][:])
-                return
-            nb = width // P
-            zw_bank = ps_w.tile([P, nb, 2, P], F32, name="zw_bank", tag="w")
-            for b in range(nb):
-                zt = chunk.tile([P, 2, P, 2], BF16, name="zt", tag="zt", align_bytes=64)
-                src = zt_banks[c0 + b * P][:].rearrange("c (u e) p -> c u p e", e=2)
-                if ZT[c] == "act":
-                    nc.scalar.copy(out=zt[:], in_=src)
-                else:
-                    nc.vector.tensor_copy(out=zt[:], in_=src)
-                pairs = zt[:].rearrange("c u p e -> c (u p e)").bitcast(F32)
+            first, width = CHUNKS[c]
+            pair_banks[c] = ps_pairs.tile([P, width // P, 2, P], F32, name="pair_bank")
+            for b in range(width // P):
+                turned = per_chunk.tile([P, 2, P, 2], BF16, name="turned", align_bytes=64)
+                nc.scalar.copy(out=turned[:], in_=sum_banks[first + b * P][:].rearrange("c (u e) p -> c u p e", e=2))
+                pairs = turned[:].rearrange("c u p e -> c (u p e)").bitcast(F32)
                 for u in range(2):
-                    nc.tensor.transpose(zw_bank[:, b, u, :], pairs[:, u * P : (u + 1) * P], ident[:])
-            nc.scalar.copy(
-                out=z[:].bitcast(F32).rearrange("p (b c u) -> p b c u", b=nb, u=2),
-                in_=zw_bank[:].rearrange("p b u c -> p b c u"),
-            )
+                    nc.tensor.transpose(pair_banks[c][:, b, u, :], pairs[:, u * P : (u + 1) * P], ident[:])
 
-        def second(c):
-            c0, width = starts[c], CHUNKS[c]
-            zc = chunk.tile([P, width], I32, name="zc", tag="zc", align_bytes=64)
-            zs = chunk.tile([P, width], U8, name="zs", tag="zs", align_bytes=64)
-            nc.vector.quantize_mx(out=zc[:].bitcast(FP8X4), scales=zs[:], in_=state[c][:])
-            res = chunk.tile([P, PACK, width], F32, name="res", tag="res", align_bytes=64)
-            rb = chunk.tile([P, width * PACK], BF16, name="rb", tag="rb", align_bytes=64)
-            per_bank = 2 if OUTIL[c] == "psum" else 512 // width
-            for t0 in range(0, PACK, per_bank):
-                bank = ps_o.tile([P, per_bank, width], F32, name="o_bank", tag="o")
-                for t in range(t0, t0 + per_bank):
-                    cols = slice(t * P, (t + 1) * P)
-                    nc.tensor.matmul_mx(
-                        out=bank[:, t - t0, :], lhsT=w2dw[:, cols].bitcast(FP8X4), lhsT_scale=w2ds[:, cols],
-                        rhs=zc[:].bitcast(FP8X4), rhs_scale=zs[:], start=True, stop=True,
-                    )
-                if OUTIL[c] == "psum":
+        def second_product(c):
+            width = CHUNKS[c][1]
+            z = per_chunk.tile([P, width * PACK], BF16, name="z", align_bytes=64)
+            if c == LAST:
+                interleave(nc.vector.tensor_copy, z[:], last_z[:])
+            else:
+                nc.scalar.copy(
+                    out=z[:].bitcast(F32).rearrange("p (b c u) -> p b c u", b=width // P, u=2),
+                    in_=pair_banks[c][:].rearrange("p b u c -> p b c u"),
+                )
+            z_w = per_chunk.tile([P, width], I32, name="z_w", align_bytes=64)
+            z_s = per_chunk.tile([P, width], U8, name="z_s", align_bytes=64)
+            nc.vector.quantize_mx(out=z_w[:].bitcast(FP8X4), scales=z_s[:], in_=z[:])
+            results[c] = per_chunk.tile([P, PACK, width], F32, name="result", align_bytes=64)
+            rounded[c] = per_chunk.tile([P, width * PACK], BF16, name="rounded", align_bytes=64)
+            slots = 2 if c == LAST else BANK // width
+            out_banks[c] = []
+            for t0 in range(0, PACK, slots):
+                bank = ps_out.tile([P, slots, width], F32, name="out_bank", tag="out")
+                out_banks[c].append((bank, slice(t0, t0 + slots)))
+                for t in range(t0, t0 + slots):
+                    multiply(bank[:, t - t0, :], w2_w, w2_s, t, z_w[:], z_s[:])
+
+        def store_result(c):
+            first, width = CHUNKS[c]
+            for bank, slots in out_banks[c]:
+                if c == LAST:
                     nc.vector.tensor_copy(
-                        out=rb[:].rearrange("p (c t) -> p c t", t=PACK)[:, :, t0 : t0 + 2], in_=bank[:].rearrange("p t c -> p c t")
+                        out=rounded[c][:].rearrange("p (c t) -> p c t", t=PACK)[:, :, slots],
+                        in_=bank[:].rearrange("p t c -> p c t"),
                     )
-                nc.scalar.copy(out=res[:, t0 : t0 + per_bank, :], in_=bank[:])
-                if OUTIL[c] == "psum":
-                    nc.scalar.dma_start(out=out_rows[:, t0 : t0 + 2, c0 : c0 + width], in_=res[:, t0 : t0 + 2, :])
-            if OUTIL[c] != "psum":
-                nc.sync.dma_start(out=out_rows[:, :, c0 : c0 + width], in_=res[:])
-            state[c] = (res, rb)
+                nc.scalar.copy(out=results[c][:, slots, :], in_=bank[:])
+                nc.sync.dma_start(out=out_rows[:, slots, first : first + width], in_=results[c][:, slots, :])
 
-        def planes(c):
-            c0, width = starts[c], CHUNKS[c]
-            cols = slice(c0, c0 + width)
-            res, rb = state[c]
-            if OUTIL[c] != "psum":
-                interleave(OUTIL[c], rb[:], res[:])
-            nc.vector.quantize_mx(out=out_codes[:, cols].bitcast(FP8X4), scales=out_scales[:, cols], in_=rb[:])
-            nc.sync.dma_start(out=out_words[:, cols], in_=out_codes[:, cols])
+        def store_codes(c):
+            first, width = CHUNKS[c]
+            cells = slice(first, first + width)
+            if c != LAST:
+                interleave(nc.vector.tensor_copy if c == 0 else nc.scalar.copy, rounded[c][:], results[c][:])
+            nc.vector.quantize_mx(out=out_codes[:, cells].bitcast(FP8X4), scales=out_scales[:, cells], in_=rounded[c][:])
+            for half in halves:
+                if half.stop == cells.stop:
+                    nc.sync.dma_start(out=words_of(out_1)[:, half], in_=out_codes[:, half])
 
-        stages = (turn_back, second, planes)
-        lag = DBUFS - 1
-        n = len(steps)
+        lag = AHEAD - 1
+        finished = [max(i for i, step in enumerate(STEPS) if step[1] == first) + lag for first, width in CHUNKS]
+        stages = [turn_back, second_product, store_result, store_codes]
         held = {}
-        for i in range(n + lag + 4):
-            for t in range(PACK):
-                if WAT[t] == i:
-                    window(t)
-            if i == 1:
-                w2dw, w2ds = deal("w2d", "xw")
-            if i < n:
-                held[i] = gather(*steps[i], SPLITLAST and i == n - 1)
-            if i < PACK and gy_cols:
-                gained(i)
-            j = i - lag
-            if 0 <= j < n:
-                pull(*steps[j], SPLITLAST and j == n - 1, *held[j])
-            for c in reversed(range(len(CHUNKS))):
-                for k in range(3):
-                    if min(POST[c][k] + lag, n + lag + 3) == i:
-                        stages[k](c)
+        for t in range(PACK - 1):
+            fetch_y(t)
+        for r in range(finished[LAST] + 1):
+            if r == 1:
+                fetch_y(PACK - 1)
+                w2_w, w2_s = deal("w2", "x_w")
+            if r < len(STEPS):
+                held[r] = differences(r)
+            if r < PACK:
+                gain_y(r)
+            if r >= lag:
+                pulls(r - lag, *held[r - lag])
+            for c in range(LAST):
+                if 0 <= r - finished[c] < len(stages):
+                    stages[r - finished[c]](c)
+        for stage in stages[1:]:
+            stage(LAST)
 
         for q in range(4):
             queue = nc.sync if q % 2 == 0 else nc.scalar
-            queue.dma_start(out=out_2[0, 4 * q : 4 * q + 4, :].bitcast(I32), in_=out_scales[32 * q : 32 * q + 4, :].bitcast(I32))
+            queue.dma_start(
+                out=out_2[0, 4 * q : 4 * q + 4, :].bitcast(I32), in_=out_scales[32 * q : 32 * q + 4, :].bitcast(I32)
+            )

@@ -55,12 +55,13 @@ def tile_picked_perona_none_po_kernel(
         x_w = keep.tile([P, T], I32, name="x_w", tag="x_w", align_bytes=64)
         x_s = keep.tile([P, T], U8, name="x_s", align_bytes=64)
         raw_w = keep.tile([P, S], I32, name="raw_w", align_bytes=64)
-        raw_s = keep.tile([P, S], U8, name="raw_s", align_bytes=64)
+        raw_s1 = keep.tile([P, S], U8, name="raw_s1", align_bytes=64)
+        raw_s2 = keep.tile([P, S], U8, name="raw_s2", align_bytes=64)
         gain = keep.tile([P, PACK], F32, name="gain")
         ident = keep.tile([P, P], F32, name="ident", align_bytes=64)
 
         nc.gpsimd.memset(x_s[:].bitcast(I32), 0)
-        nc.gpsimd.memset(raw_s[:].bitcast(I32), 0)
+        nc.gpsimd.memset(raw_s1[:].bitcast(I32), 0)
 
         nc.scalar.dma_start(out=gain[:], in_=gn.rearrange("(p t) o -> p (t o)", t=PACK))
         nc.sync.dma_start(offs_t[:], offs)
@@ -69,24 +70,25 @@ def tile_picked_perona_none_po_kernel(
         nc.sync.dma_start(out=raw_w[:], in_=words_of(w1_words))
         nc.sync.dma_start(out=x_w[:], in_=words_of(x_words))
         load_scales([nc.scalar] * 4, x_s, x_scales)
-        load_scales([nc.gpsimd, nc.scalar, nc.scalar, nc.scalar], raw_s, w1_scales)
+        load_scales([nc.gpsimd, nc.scalar, nc.scalar, nc.scalar], raw_s1, w1_scales)
         make_identity(nc, ident[:])
+        nc.gpsimd.memset(raw_s2[:].bitcast(I32), 0)
 
-        def deal(name, tag):
+        def deal(name, tag, raw_s, byte_engine):
             words = keep.tile([P, S], I32, name=name + "_w", tag=tag, align_bytes=64)
             scales = keep.tile([P, S], U8, name=name + "_s", align_bytes=64)
             nc.vector.tensor_copy(
                 out=words[:].rearrange("p (t a b) -> p a t b", t=PACK, b=4),
                 in_=raw_w[:].rearrange("p (a b t) -> p a t b", t=PACK, b=4),
             )
-            nc.vector.tensor_copy(
+            byte_engine.tensor_copy(
                 out=scales[:].rearrange("p (t m) -> p t m", t=PACK), in_=raw_s[:].rearrange("p (m t) -> p t m", t=PACK)
             )
             return words, scales
 
-        w1_w, w1_s = deal("w1", "w1_w")
+        w1_w, w1_s = deal("w1", "w1_w", raw_s1, nc.gpsimd)
         nc.sync.dma_start(out=raw_w[:], in_=words_of(w2_words))
-        load_scales([nc.sync] * 4, raw_s, w2_scales)
+        load_scales([nc.sync] * 4, raw_s2, w2_scales)
 
         halves = [slice(0, HALF), slice(HALF, S)]
         picked_s = keep.tile([P, S], U8, name="picked_s", align_bytes=64)
@@ -257,7 +259,7 @@ def tile_picked_perona_none_po_kernel(
         for r in range(finished[LAST] + 1):
             if r == 1:
                 fetch_y(PACK - 1)
-                w2_w, w2_s = deal("w2", "x_w")
+                w2_w, w2_s = deal("w2", "x_w", raw_s2, nc.vector)
             if r < len(STEPS):
                 held[r] = differences(r)
             if r < PACK:

from contextlib import ExitStack

import concourse.mybir as mybir
from concourse.masks import make_identity

F32 = mybir.dt.float32
BF16 = mybir.dt.bfloat16
I32 = mybir.dt.int32
U32 = mybir.dt.uint32
U16 = mybir.dt.uint16
U8 = mybir.dt.uint8
FP8X4 = mybir.dt.float8_e4m3fn_x4
ALU = mybir.AluOpType
ACT = mybir.ActivationFunctionType

P = 128
PACK = 4
T = 2048
S = 512
HALF = S // 2
BANK = 512
PER_COLUMN = 16
FLOPS = 2 * 2 * S * S * S

CHUNKS = [(0, HALF), (HALF, P), (HALF + P, P)]
LAST = len(CHUNKS) - 1
STEPS = [(t, 0, HALF) for t in range(PACK)] + [(0, HALF, HALF)]
STEPS = STEPS + [(t, first, width) for first, width in CHUNKS[1:] for t in range(1, PACK)]
AHEAD = 3


def tile_picked_perona_none_po_kernel(
    tc, x_words, x_scales, w1_words, w1_scales, gn, w2_words, w2_scales, offs, p1, p2, out_0, out_1, out_2
):
    nc = tc.nc
    with ExitStack() as ctx:
        keep = ctx.enter_context(tc.tile_pool(name="keep", bufs=1))
        per_chunk = ctx.enter_context(tc.tile_pool(name="per_chunk", bufs=len(CHUNKS)))
        ps_sum = ctx.enter_context(tc.psum_pool(name="ps_sum", bufs=4))
        ps_pairs = ctx.enter_context(tc.psum_pool(name="ps_pairs", bufs=1))
        ps_out = ctx.enter_context(tc.psum_pool(name="ps_out", bufs=3))

        def words_of(packed):
            return packed[0].rearrange("p n t -> p (n t)").bitcast(I32)

        def load_scales(queues, plane, scales):
            for q, queue in enumerate(queues):
                queue.dma_start(
                    out=plane[32 * q : 32 * q + 4, :].bitcast(I32), in_=scales[0, 4 * q : 4 * q + 4, :].bitcast(I32)
                )

        offs_t = keep.tile([P, S // PER_COLUMN], U16, name="offs_t")
        p1_t = keep.tile([P, S // PER_COLUMN], U16, name="p1_t")
        p2_t = keep.tile([P, S // PER_COLUMN], U16, name="p2_t")
        x_w = keep.tile([P, T], I32, name="x_w", tag="x_w", align_bytes=64)
        x_s = keep.tile([P, T], U8, name="x_s", align_bytes=64)
        raw_w = keep.tile([P, S], I32, name="raw_w", align_bytes=64)
        raw_s1 = keep.tile([P, S], U8, name="raw_s1", align_bytes=64)
        raw_s2 = keep.tile([P, S], U8, name="raw_s2", align_bytes=64)
        gain = keep.tile([P, PACK], F32, name="gain")
        ident = keep.tile([P, P], F32, name="ident", align_bytes=64)

        nc.gpsimd.memset(x_s[:].bitcast(I32), 0)
        nc.gpsimd.memset(raw_s1[:].bitcast(I32), 0)

        nc.scalar.dma_start(out=gain[:], in_=gn.rearrange("(p t) o -> p (t o)", t=PACK))
        nc.sync.dma_start(offs_t[:], offs)
        nc.sync.dma_start(p1_t[:], p1)
        nc.sync.dma_start(p2_t[:], p2)
        nc.sync.dma_start(out=raw_w[:], in_=words_of(w1_words))
        nc.sync.dma_start(out=x_w[:], in_=words_of(x_words))
        load_scales([nc.scalar] * 4, x_s, x_scales)
        load_scales([nc.gpsimd, nc.scalar, nc.scalar, nc.scalar], raw_s1, w1_scales)
        make_identity(nc, ident[:])
        nc.gpsimd.memset(raw_s2[:].bitcast(I32), 0)

        def deal(name, tag, raw_s, byte_engine):
            words = keep.tile([P, S], I32, name=name + "_w", tag=tag, align_bytes=64)
            scales = keep.tile([P, S], U8, name=name + "_s", align_bytes=64)
            nc.vector.tensor_copy(
                out=words[:].rearrange("p (t a b) -> p a t b", t=PACK, b=4),
                in_=raw_w[:].rearrange("p (a b t) -> p a t b", t=PACK, b=4),
            )
            byte_engine.tensor_copy(
                out=scales[:].rearrange("p (t m) -> p t m", t=PACK), in_=raw_s[:].rearrange("p (m t) -> p t m", t=PACK)
            )
            return words, scales

        w1_w, w1_s = deal("w1", "w1_w", raw_s1, nc.gpsimd)
        nc.sync.dma_start(out=raw_w[:], in_=words_of(w2_words))
        load_scales([nc.sync] * 4, raw_s2, w2_scales)

        halves = [slice(0, HALF), slice(HALF, S)]
        picked_s = keep.tile([P, S], U8, name="picked_s", align_bytes=64)
        picked_w = keep.tile([P, S], U32, name="picked_w", align_bytes=64)
        nc.vector.tensor_copy(out=picked_s[:], in_=x_s[:].indirect(offs_t[:]))
        for cells in halves:
            entries = slice(cells.start // PER_COLUMN, cells.stop // PER_COLUMN)
            nc.vector.tensor_copy(out=picked_w[:, cells], in_=x_w[:].bitcast(U32).indirect(offs_t[:, entries]))

        quarter_gain = keep.tile([P, PACK], F32, name="quarter_gain")
        nc.vector.tensor_scalar(out=quarter_gain[:], in0=gain[:], scalar1=0.25, scalar2=0.0, op0=ALU.mult, op1=ALU.add)

        y = [keep.tile([P, S], F32, name="y%d" % t, align_bytes=64) for t in range(PACK)]
        y_twin = [keep.tile([P, S], F32, name="y_twin%d" % t, align_bytes=64) for t in range(PACK)]
        gained_y = [keep.tile([P, S], F32, name="gained_y%d" % t, align_bytes=64) for t in range(PACK)]

        def multiply(bank, words, scales, t, moving_words, moving_scales):
            columns = slice(t * P, (t + 1) * P)
            nc.tensor.matmul_mx(
                out=bank, lhsT=words[:, columns].bitcast(FP8X4), lhsT_scale=scales[:, columns],
                rhs=moving_words.bitcast(FP8X4), rhs_scale=moving_scales, start=True, stop=True,
            )

        y_banks = [
            [ps_out.tile([P, HALF], F32, name="y_bank", tag="out"), ps_sum.tile([P, HALF], F32, name="y_bank", tag="sum")]
        ]
        for bank, cells in zip(y_banks[0], halves):
            multiply(bank[:], w1_w, w1_s, 0, picked_w[:, cells], picked_s[:, cells])
        for t in range(1, PACK):
            y_banks.append(ps_sum.tile([P, S], F32, name="y_bank", tag="sum"))
            multiply(y_banks[t][:], w1_w, w1_s, t, picked_w[:], picked_s[:])

        def fetch_y(t):
            if t == 0:
                nc.scalar.copy(out=y[0][:, halves[0]], in_=y_banks[0][0][:])
                nc.vector.tensor_copy(out=y_twin[0][:, halves[0]], in_=y[0][:, halves[0]])
                nc.scalar.copy(out=y[0][:, halves[1]], in_=y_banks[0][1][:])
            else:
                nc.scalar.copy(out=y[t][:], in_=y_banks[t][:])
                nc.scalar.copy(out=y_twin[t][:, halves[0]], in_=y_banks[t][:, halves[0]])
            nc.sync.dma_start(out=y_twin[t][:, halves[1]], in_=y[t][:, halves[1]])

        def gain_y(t):
            cells = slice(0, CHUNKS[LAST][0])
            nc.scalar.activation(out=gained_y[t][:, cells], in_=y[t][:, cells], func=ACT.Copy, scale=gain[:, t : t + 1])

        scratch = [keep.tile([P, S], F32, name="scratch%d" % i, align_bytes=64) for i in range(len(STEPS) + AHEAD)]
        last_cells = slice(CHUNKS[LAST][0], S)
        last_z = keep.tile([P, PACK, P], F32, name="last_z", align_bytes=64)
        sum_banks = {}

        def differences(i):
            t, first, width = STEPS[i]
            d = scratch[i][:, : 2 * width].rearrange("p (l w) -> p l w", l=2)
            square = scratch[i + AHEAD][:, : 2 * width].rearrange("p (l w) -> p l w", l=2)
            e = keep.tile([P, 2, width], F32, name="e%d" % i, align_bytes=64)
            entries = slice(first // PER_COLUMN, (first + width) // PER_COLUMN)
            by_list = i == len(STEPS) - 1
            for l, lists in enumerate((p1_t, p2_t)):
                nc.vector.tensor_tensor(
                    out=d[:, l, :], in0=y[t][:].indirect(lists[:, entries]), in1=y_twin[t][:, first : first + width],
                    op=ALU.subtract,
                )
                if by_list:
                    nc.scalar.activation(out=square[:, l, :], in_=d[:, l, :], func=ACT.Square)
                    nc.scalar.activation(out=e[:, l, :], in_=square[:, l, :], func=ACT.Exp, scale=-0.5)
            if not by_list:
                nc.scalar.activation(out=square, in_=d, func=ACT.Square)
                nc.scalar.activation(out=e[:], in_=square, func=ACT.Exp, scale=-0.5)
            return d, e

        def pulls(i, d, e):
            t, first, width = STEPS[i]
            pull = keep.tile([P, 2, width], F32, name="pull%d" % i, align_bytes=64)
            g, g4 = gain[:, t : t + 1], quarter_gain[:, t : t + 1]
            if i == len(STEPS) - 1:
                part = keep.tile([P, P], F32, name="part%d" % i, align_bytes=64)
                nc.vector.scalar_tensor_tensor(out=pull[:, 0, :], in0=e[:, 0, :], scalar=g4, in1=d[:, 0, :], op0=ALU.mult, op1=ALU.mult)
                nc.vector.scalar_tensor_tensor(out=part[:], in0=y[t][:, last_cells], scalar=g, in1=pull[:, 0, :], op0=ALU.mult, op1=ALU.add)
                nc.vector.tensor_tensor(out=pull[:, 1, :], in0=e[:, 1, :], in1=d[:, 1, :], op=ALU.mult)
                nc.vector.scalar_tensor_tensor(out=last_z[:, t, :], in0=pull[:, 1, :], scalar=g4, in1=part[:], op0=ALU.mult, op1=ALU.add)
                return
            nc.vector.scalar_tensor_tensor(out=pull[:], in0=e[:], scalar=g4, in1=d, op0=ALU.mult, op1=ALU.mult)
            for block in range(first, first + width, P):
                mine = slice(block - first, block - first + P)
                if block == last_cells.start:
                    part = keep.tile([P, P], F32, name="part%d" % i, align_bytes=64)
                    nc.vector.scalar_tensor_tensor(out=part[:], in0=y[t][:, last_cells], scalar=g, in1=pull[:, 0, mine], op0=ALU.mult, op1=ALU.add)
                    nc.vector.tensor_tensor(out=last_z[:, t, :], in0=part[:], in1=pull[:, 1, mine], op=ALU.add)
                    continue
                if t == 0:
                    sum_banks[block] = ps_sum.tile([P, PACK, P], F32, name="sum_bank", tag="sum")
                terms = (pull[:, 0, mine], pull[:, 1, mine], gained_y[t][:, block : block + P])
                for k, term in enumerate(terms):
                    nc.tensor.matmul(
                        sum_banks[block][:, t, :], lhsT=term, rhs=ident[:], is_transpose=True,
                        start=(k == 0), stop=(k == len(terms) - 1),
                    )

        out_codes = keep.tile([P, S], I32, name="out_codes", align_bytes=64)
        out_scales = keep.tile([P, S], U8, name="out_scales", align_bytes=64)
        out_rows = out_0.rearrange("(p t) j -> p t j", t=PACK)
        pair_banks, out_banks, results, rounded = {}, {}, {}, {}

        def interleave(copy, dst, src):
            copy(out=dst.rearrange("p (c t) -> p c t", t=PACK), in_=src.rearrange("p t c -> p c t"))

        def turn_back(c):
            first, width = CHUNKS[c]
            pair_banks[c] = ps_pairs.tile([P, width // P, 2, P], F32, name="pair_bank")
            for b in range(width // P):
                turned = per_chunk.tile([P, 2, P, 2], BF16, name="turned", align_bytes=64)
                nc.scalar.copy(out=turned[:], in_=sum_banks[first + b * P][:].rearrange("c (u e) p -> c u p e", e=2))
                pairs = turned[:].rearrange("c u p e -> c (u p e)").bitcast(F32)
                for u in range(2):
                    nc.tensor.transpose(pair_banks[c][:, b, u, :], pairs[:, u * P : (u + 1) * P], ident[:])

        def second_product(c):
            width = CHUNKS[c][1]
            z = per_chunk.tile([P, width * PACK], BF16, name="z", align_bytes=64)
            if c == LAST:
                interleave(nc.vector.tensor_copy, z[:], last_z[:])
            else:
                nc.scalar.copy(
                    out=z[:].bitcast(F32).rearrange("p (b c u) -> p b c u", b=width // P, u=2),
                    in_=pair_banks[c][:].rearrange("p b u c -> p b c u"),
                )
            z_w = per_chunk.tile([P, width], I32, name="z_w", align_bytes=64)
            z_s = per_chunk.tile([P, width], U8, name="z_s", align_bytes=64)
            nc.vector.quantize_mx(out=z_w[:].bitcast(FP8X4), scales=z_s[:], in_=z[:])
            results[c] = per_chunk.tile([P, PACK, width], F32, name="result", align_bytes=64)
            rounded[c] = per_chunk.tile([P, width * PACK], BF16, name="rounded", align_bytes=64)
            slots = 2 if c == LAST else BANK // width
            out_banks[c] = []
            for t0 in range(0, PACK, slots):
                bank = ps_out.tile([P, slots, width], F32, name="out_bank", tag="out")
                out_banks[c].append((bank, slice(t0, t0 + slots)))
                for t in range(t0, t0 + slots):
                    multiply(bank[:, t - t0, :], w2_w, w2_s, t, z_w[:], z_s[:])

        def store_result(c):
            first, width = CHUNKS[c]
            for bank, slots in out_banks[c]:
                if c == LAST:
                    nc.vector.tensor_copy(
                        out=rounded[c][:].rearrange("p (c t) -> p c t", t=PACK)[:, :, slots],
                        in_=bank[:].rearrange("p t c -> p c t"),
                    )
                nc.scalar.copy(out=results[c][:, slots, :], in_=bank[:])
                nc.sync.dma_start(out=out_rows[:, slots, first : first + width], in_=results[c][:, slots, :])

        def store_codes(c):
            first, width = CHUNKS[c]
            cells = slice(first, first + width)
            if c != LAST:
                interleave(nc.vector.tensor_copy if c == 0 else nc.scalar.copy, rounded[c][:], results[c][:])
            nc.vector.quantize_mx(out=out_codes[:, cells].bitcast(FP8X4), scales=out_scales[:, cells], in_=rounded[c][:])
            for half in halves:
                if half.stop == cells.stop:
                    nc.sync.dma_start(out=words_of(out_1)[:, half], in_=out_codes[:, half])

        lag = AHEAD - 1
        finished = [max(i for i, step in enumerate(STEPS) if step[1] == first) + lag for first, width in CHUNKS]
        stages = [turn_back, second_product, store_result, store_codes]
        held = {}
        for t in range(PACK - 1):
            fetch_y(t)
        for r in range(finished[LAST] + 1):
            if r == 1:
                fetch_y(PACK - 1)
                w2_w, w2_s = deal("w2", "x_w", raw_s2, nc.vector)
            if r < len(STEPS):
                held[r] = differences(r)
            if r < PACK:
                gain_y(r)
            if r >= lag:
                pulls(r - lag, *held[r - lag])
            for c in range(LAST):
                if 0 <= r - finished[c] < len(stages):
                    stages[r - finished[c]](c)
        for stage in stages[1:]:
            stage(LAST)

        for q in range(4):
            queue = nc.sync if q % 2 == 0 else nc.scalar
            queue.dma_start(
                out=out_2[0, 4 * q : 4 * q + 4, :].bitcast(I32), in_=out_scales[32 * q : 32 * q + 4, :].bitcast(I32)
            )
